import numpy as np
import ml_dtypes


def mxq(x, axis, fmt="e4m3"):
    dtype, down = {"e4m3": (ml_dtypes.float8_e4m3fn, 7), "e5m2": (ml_dtypes.float8_e5m2, 14)}[fmt]
    v = np.moveaxis(np.asarray(x, np.float32).astype(ml_dtypes.bfloat16).astype(np.float64), axis, -1)
    blocks = v.reshape(v.shape[:-1] + (-1, 32))
    amax = np.abs(blocks).max(-1, keepdims=True)
    byte = np.maximum(np.where(amax > 0, np.frexp(amax)[1] - 1 + 127, 0) - down, 1)
    scale = np.exp2(byte - 127.0)
    codes = (blocks / scale).astype(np.float32).astype(dtype).astype(np.float64)
    return np.moveaxis((codes * scale).reshape(v.shape), -1, axis)


WIDE = False


def mx_kscale(k):
    if not WIDE:
        return np.ones(k)
    levels = np.array([10, -10, 5, -5, 0])
    if k % 512:
        return np.exp2(np.random.permutation(np.resize(levels, k // 32))).repeat(32)
    a = np.empty((k // 512, 16))
    for p in range(k // 512):
        a[p, :8] = np.random.permutation(np.resize(levels, 8))
        for g in range(8):
            far = levels[np.abs(levels - a[p, g]) >= 10]
            a[p, g + 8] = far[np.random.randint(len(far))]
    return np.exp2(a.ravel()).repeat(32)


def f64(x):
    return np.asarray(x).astype(np.float64)


def striped(idx):
    return np.tile(np.asarray(idx).reshape(-1, 16).T, (8, 1)).astype(np.uint16)


def unstriped(offs):
    return offs[:16].T.reshape(-1).astype(np.int64)


E2M1 = np.array([0.0, 0.5, 1.0, 1.5, 2.0, 3.0, 4.0, 6.0, -0.0, -0.5, -1.0, -1.5, -2.0, -3.0, -4.0, -6.0])


def pack_weight(w, fmt):
    k, n = w.shape
    w = f64(np.asarray(w, np.float32).astype(ml_dtypes.bfloat16)).reshape(k // 32, 32, n)
    amax = np.abs(w).max(1)
    if fmt == "e4m3":
        byte = np.frexp(amax)[1] - 1 + 127 - 7
    else:
        mant, ex = np.frexp(amax / 6.0)
        byte = np.where(mant > 0.5, ex, ex - 1) + 127
    byte = np.clip(np.where(amax > 0, byte, 1), 1, 254)
    scaled = (w * np.exp2(127.0 - byte)[:, None, :]).reshape(k, n).astype(np.float32)
    by_word = np.ascontiguousarray(scaled.reshape(k // 512, 128, 4, n).transpose(0, 1, 3, 2))
    if fmt == "e4m3":
        words = by_word.astype(ml_dtypes.float8_e4m3fn).view(np.uint8)
    else:
        c = by_word.astype(ml_dtypes.float4_e2m1fn).view(np.uint8) & 0xF
        words = (c[..., 0::2] | (c[..., 1::2] << 4)).reshape(k // 512, 128, 2 * n)
    return np.ascontiguousarray(words), np.ascontiguousarray(byte.astype(np.uint8).reshape(k // 512, 16, n))


def unpack_weight(words, scales, fmt):
    g, _, n = scales.shape
    words = np.ascontiguousarray(words).reshape(g, 128, n, -1)
    if fmt == "e4m3":
        vals = words.view(ml_dtypes.float8_e4m3fn).astype(np.float64)
    else:
        nib = np.empty((g, 128, n, 4), np.uint8)
        nib[..., 0::2] = words & 0xF
        nib[..., 1::2] = words >> 4
        vals = E2M1[nib]
    vals = vals * np.repeat(np.exp2(scales.astype(np.float64) - 127.0), 8, axis=1)[..., None]
    return vals.transpose(0, 1, 3, 2).reshape(g * 512, n)


D, E, T, I, Q = 512, 512, 2048, 512, 128


def setup_inputs():
    n = np.random.standard_normal
    idx = np.random.permutation(T)[:I]
    fd = mx_kscale(D)
    fe = mx_kscale(E)
    keysp = pack_weight(n((D, T)) / fd[:, None], "e2m1")
    valsp = pack_weight(n((E, T)) / fe[:, None], "e2m1")
    return {
        "query": (n((D, Q)) * 0.4 / np.sqrt(D) * fd[:, None]).astype(np.float32),
        "query2": (n((D, Q)) * 0.5 / np.sqrt(D) * fd[:, None]).astype(np.float32),
        "keys_words": keysp[0],
        "keys_scales": keysp[1],
        "gout": (n((E, Q)) * 1 / np.sqrt(E) * fe[:, None]).astype(np.float32),
        "vals_words": valsp[0],
        "vals_scales": valsp[1],
        "size": (np.random.uniform(0.5, 2.0, (1, I))).astype(np.float32),
        "old": (0.5 * n((Q, T))).astype(np.float32),
        "offs": striped(idx),
    }


def reference(query, query2, keys_words, keys_scales, gout, vals_words, vals_scales, size, old, offs):
    idx = unstriped(offs)
    keysu = unpack_weight(keys_words, keys_scales, "e2m1")
    valsu = unpack_weight(vals_words, vals_scales, "e2m1")
    queryq = mxq(f64(query), 0, "e4m3")
    keysidxg = keysu[:, idx]
    a = queryq.T @ keysidxg
    query2q = mxq(f64(query2), 0, "e4m3")
    b = query2q.T @ keysidxg
    s = a * (b + 1.0)
    p = np.exp(s - np.max(s, axis=1, keepdims=True))
    z = np.sum(p, axis=1, keepdims=True)
    goutq = mxq(f64(gout), 0, "e4m3")
    valsidxg = valsu[:, idx]
    c0 = goutq.T @ valsidxg
    dz = np.sum(c0 * p * f64(size) / np.square(z) * (-1.0), axis=1, keepdims=True)
    dp = c0 / z * f64(size) + dz
    ds = dp * p
    da = ds * (b + 1.0)
    gs = da * 512.0
    gf = np.zeros((Q, T))
    gf[:, idx] = gs
    y = f64(old) + gf
    return y

@@ -1,0 +1,151 @@
+from contextlib import ExitStack
+
+import concourse.mybir as mybir
+from concourse.masks import make_identity
+
+D, E, T, I, Q = 512, 512, 2048, 512, 128
+FLOPS = 3 * 2 * D * Q * I
+
+F32 = mybir.dt.float32
+BF16 = mybir.dt.bfloat16
+I32 = mybir.dt.int32
+U32 = mybir.dt.uint32
+U16 = mybir.dt.uint16
+U8 = mybir.dt.uint8
+FP8X4 = mybir.dt.float8_e4m3fn_x4
+FP4X4 = mybir.dt.float4_e2m1fn_x4
+ALU = mybir.AluOpType
+ACT = mybir.ActivationFunctionType
+
+P = 128
+PACK = 4
+OUT_WIDTHS = (128, 384, 512, 512, 256, 256)
+
+
+def tile_attend_bproductscore_a_s_kernel(tc, query, query2, keys_words, keys_scales, gout, vals_words, vals_scales, size, old, offs, out):
+    nc = tc.nc
+    with ExitStack() as ctx:
+        sb = ctx.enter_context(tc.tile_pool(name="sb", bufs=1))
+        ps = ctx.enter_context(tc.psum_pool(name="ps", bufs=1))
+
+        offsets = sb.tile([P, I // 16], U16, name="offsets")
+        nc.sync.dma_start(offsets[:], offs)
+
+        def scale_pool(name):
+            pool = sb.tile([P, T], U8, name=name)
+            nc.vector.memset(pool[:].bitcast(I32), 0)
+            return pool
+
+        def load_scales(pool, scales):
+            for r in range(4):
+                nc.sync.dma_start(pool[r:P:32, :].bitcast(I32), scales[0, r:16:4, :].bitcast(I32))
+
+        def load_words(name, words, tag):
+            pool = sb.tile([P, T], U16, name=name, tag=tag, align_bytes=64)
+            nc.sync.dma_start(pool[:].bitcast(I32), words[0].bitcast(I32))
+            return pool
+
+        def load_rows(name, x):
+            raw = sb.tile([P, PACK, Q], F32, name=name)
+            nc.sync.dma_start(raw[:], x.rearrange("(p j) q -> p j q", j=PACK))
+            return raw
+
+        def interleave(name, raw, tag):
+            grouped = sb.tile([P, Q, PACK], BF16, name=name, tag=tag, align_bytes=64)
+            nc.scalar.copy(grouped[:], raw[:].rearrange("p j q -> p q j"))
+            return grouped
+
+        def quantize(name, grouped):
+            codes = sb.tile([P, Q], U32, name=name + "_codes", align_bytes=64)
+            scales = sb.tile([P, Q], U8, name=name + "_scales", align_bytes=64)
+            nc.vector.quantize_mx(out=codes[:].bitcast(FP8X4), scales=scales[:], in_=grouped[:].rearrange("p q j -> p (q j)"))
+            return codes, scales
+
+        def gather(name, pool, dtype, tag):
+            listed = sb.tile([P, I], dtype, name=name, tag=tag, align_bytes=64)
+            nc.vector.tensor_copy(listed[:], pool[:].indirect(offsets[:]))
+            return listed
+
+        def product(name, rows, words, scales):
+            bank = ps.tile([Q, I], F32, name=name)
+            nc.tensor.matmul_mx(out=bank[:], lhsT=rows[0][:].bitcast(FP8X4), lhsT_scale=rows[1][:],
+                                rhs=words[:].bitcast(FP4X4), rhs_scale=scales[:], start=True, stop=True)
+            return bank
+
+        key_scale_pool = sb.tile([P, T], U8, name="key_scale_pool")
+        nc.vector.memset(key_scale_pool[:, : T // 2].bitcast(I32), 0)
+        nc.gpsimd.memset(key_scale_pool[:, T // 2 :].bitcast(I32), 0)
+        val_scale_pool = scale_pool("val_scale_pool")
+        scattered = sb.tile([Q, T], F32, name="scattered")
+        nc.vector.memset(scattered[:].bitcast(I32), 0)
+
+        load_scales(key_scale_pool, keys_scales)
+        key_word_pool = load_words("key_word_pool", keys_words, "key_word_pool")
+        query2_raw = load_rows("query2_raw", query2)
+        query_raw = load_rows("query_raw", query)
+        size_cols = sb.tile([P, PACK], F32, name="size_cols")
+        nc.sync.dma_start(size_cols[:], size.rearrange("o (p j) -> (o p) j", j=PACK))
+        val_word_pool = load_words("val_word_pool", vals_words, "wide")
+        gout_raw = load_rows("gout_raw", gout)
+        load_scales(val_scale_pool, vals_scales)
+        old_sb = sb.tile([Q, T], F32, name="old_sb")
+        nc.sync.dma_start(old_sb[:], old)
+
+        identity = sb.tile([P, P], F32, name="identity")
+        make_identity(nc, identity[:])
+
+        warm = sb.tile([P, 1], F32, name="warm")
+        nc.scalar.activation(warm[:], identity[:, 0:1], ACT.Exp)
+
+        query2_bf = interleave("query2_bf", query2_raw, "query2_bf")
+        query_bf = interleave("query_bf", query_raw, "query_bf")
+
+        key_words = gather("key_words", key_word_pool, U16, "key_words")
+        key_scales = gather("key_scales", key_scale_pool, U8, "key_scales")
+        query2_mx = quantize("query2", query2_bf)
+        query_mx = quantize("query", query_bf)
+        b = product("b", query2_mx, key_words, key_scales)
+        a = product("a", query_mx, key_words, key_scales)
+        size_rows = ps.tile([Q, PACK, P], F32, name="size_rows")
+        for j in range(PACK):
+            nc.tensor.transpose(size_rows[:, j, :], size_cols[:, j : j + 1].to_broadcast([P, P]), identity[:])
+        val_words = gather("val_words", val_word_pool, U16, "query_bf")
+
+        b1 = sb.tile([Q, I], F32, name="b1")
+        nc.scalar.activation(b1[:], b[:], ACT.Copy, bias=1.0)
+        gout_bf = interleave("gout_bf", gout_raw, "key_words")
+        s = sb.tile([Q, I], F32, name="s", tag="wide", align_bytes=64)
+        nc.vector.tensor_tensor(s[:], a[:], b1[:], ALU.mult)
+        gout_mx = quantize("gout", gout_bf)
+        neg_s = sb.tile([Q, I], F32, name="neg_s", tag="key_words", align_bytes=64)
+        neg_max = sb.tile([Q, 1], F32, name="neg_max")
+        nc.vector.tensor_scalar(neg_s[:], s[:], -1.0, None, ALU.mult, ALU.min, accum_out=neg_max[:])
+        p = sb.tile([Q, I], F32, name="p")
+        z = sb.tile([Q, 1], F32, name="z")
+        nc.scalar.activation(p[:], neg_s[:], ACT.Exp, bias=neg_max[:], scale=-1.0, accum_out=z[:])
+
+        val_scales = gather("val_scales", val_scale_pool, U8, "wide")
+        c0 = product("c0", gout_mx, val_words, val_scales)
+
+        rz = sb.tile([Q, 1], F32, name="rz")
+        nc.vector.reciprocal(rz[:], z[:])
+        pn = sb.tile([Q, I], F32, name="pn")
+        nc.scalar.activation(pn[:], p[:], ACT.Copy, scale=rz[:])
+        pn_size = sb.tile([Q, P, PACK], F32, name="pn_size")
+        nc.vector.scalar_tensor_tensor(pn_size[:], p[:].rearrange("q (n j) -> q n j", j=PACK), rz[:],
+                                       size_rows[:].rearrange("q j n -> q n j"), ALU.mult, ALU.mult)
+        direct = sb.tile([Q, I], F32, name="direct")
+        direct_sum = sb.tile([Q, 1], F32, name="direct_sum")
+        nc.vector.scalar_tensor_tensor(direct[:], c0[:], -512.0, pn_size[:].rearrange("q n j -> q (n j)"),
+                                       ALU.mult, ALU.mult, accum_out=direct_sum[:])
+        ds = sb.tile([Q, I], F32, name="ds")
+        nc.vector.scalar_tensor_tensor(ds[:], pn[:], direct_sum[:], direct[:], ALU.mult, ALU.subtract)
+        nc.vector.tensor_tensor(scattered[:].indirect(offsets[:]), ds[:], b1[:], ALU.mult)
+
+        start = 0
+        for k, width in enumerate(OUT_WIDTHS):
+            cols = slice(start, start + width)
+            start = start + width
+            total = sb.tile([Q, width], F32, name="total%d" % k)
+            nc.vector.tensor_tensor(total[:], scattered[:, cols], old_sb[:, cols], ALU.add)
+            nc.sync.dma_start(out[:, cols], total[:])

@@ -19,7 +19,7 @@ ACT = mybir.ActivationFunctionType
 
 P = 128
 PACK = 4
-OUT_WIDTHS = (128, 384, 512, 512, 256, 256)
+OUT_CHUNK = 256
 
 
 def tile_attend_bproductscore_a_s_kernel(tc, query, query2, keys_words, keys_scales, gout, vals_words, vals_scales, size, old, offs, out):
@@ -40,8 +40,8 @@ def tile_attend_bproductscore_a_s_kernel(tc, query, query2, keys_words, keys_sca
             for r in range(4):
                 nc.sync.dma_start(pool[r:P:32, :].bitcast(I32), scales[0, r:16:4, :].bitcast(I32))
 
-        def load_words(name, words, tag):
-            pool = sb.tile([P, T], U16, name=name, tag=tag, align_bytes=64)
+        def load_words(name, words):
+            pool = sb.tile([P, T], U16, name=name)
             nc.sync.dma_start(pool[:].bitcast(I32), words[0].bitcast(I32))
             return pool
 
@@ -50,9 +50,9 @@ def tile_attend_bproductscore_a_s_kernel(tc, query, query2, keys_words, keys_sca
             nc.sync.dma_start(raw[:], x.rearrange("(p j) q -> p j q", j=PACK))
             return raw
 
-        def interleave(name, raw, tag):
-            grouped = sb.tile([P, Q, PACK], BF16, name=name, tag=tag, align_bytes=64)
-            nc.scalar.copy(grouped[:], raw[:].rearrange("p j q -> p q j"))
+        def interleave(name, raw):
+            grouped = sb.tile([P, Q, PACK], BF16, name=name, align_bytes=64)
+            nc.scalar.copy(grouped[:].rearrange("p (c i) j -> p c j i", i=4), raw[:].rearrange("p j (c i) -> p c j i", i=4))
             return grouped
 
         def quantize(name, grouped):
@@ -61,8 +61,8 @@ def tile_attend_bproductscore_a_s_kernel(tc, query, query2, keys_words, keys_sca
             nc.vector.quantize_mx(out=codes[:].bitcast(FP8X4), scales=scales[:], in_=grouped[:].rearrange("p q j -> p (q j)"))
             return codes, scales
 
-        def gather(name, pool, dtype, tag):
-            listed = sb.tile([P, I], dtype, name=name, tag=tag, align_bytes=64)
+        def gather(name, pool, dtype):
+            listed = sb.tile([P, I], dtype, name=name, align_bytes=64)
             nc.vector.tensor_copy(listed[:], pool[:].indirect(offsets[:]))
             return listed
 
@@ -72,80 +72,75 @@ def tile_attend_bproductscore_a_s_kernel(tc, query, query2, keys_words, keys_sca
                                 rhs=words[:].bitcast(FP4X4), rhs_scale=scales[:], start=True, stop=True)
             return bank
 
-        key_scale_pool = sb.tile([P, T], U8, name="key_scale_pool")
-        nc.vector.memset(key_scale_pool[:, : T // 2].bitcast(I32), 0)
-        nc.gpsimd.memset(key_scale_pool[:, T // 2 :].bitcast(I32), 0)
+        key_scale_pool = scale_pool("key_scale_pool")
         val_scale_pool = scale_pool("val_scale_pool")
         scattered = sb.tile([Q, T], F32, name="scattered")
         nc.vector.memset(scattered[:].bitcast(I32), 0)
 
-        load_scales(key_scale_pool, keys_scales)
-        key_word_pool = load_words("key_word_pool", keys_words, "key_word_pool")
-        query2_raw = load_rows("query2_raw", query2)
-        query_raw = load_rows("query_raw", query)
         size_cols = sb.tile([P, PACK], F32, name="size_cols")
         nc.sync.dma_start(size_cols[:], size.rearrange("o (p j) -> (o p) j", j=PACK))
-        val_word_pool = load_words("val_word_pool", vals_words, "wide")
-        gout_raw = load_rows("gout_raw", gout)
+        key_word_pool = load_words("key_word_pool", keys_words)
+        query2_raw = load_rows("query2_raw", query2)
+        load_scales(key_scale_pool, keys_scales)
+        query_raw = load_rows("query_raw", query)
         load_scales(val_scale_pool, vals_scales)
+        gout_raw = load_rows("gout_raw", gout)
+        val_word_pool = load_words("val_word_pool", vals_words)
         old_sb = sb.tile([Q, T], F32, name="old_sb")
         nc.sync.dma_start(old_sb[:], old)
 
         identity = sb.tile([P, P], F32, name="identity")
         make_identity(nc, identity[:])
+        size_rows = ps.tile([Q, PACK, P], F32, name="size_rows")
+        for j in range(PACK):
+            nc.tensor.transpose(size_rows[:, j, :], size_cols[:, j : j + 1].to_broadcast([P, P]), identity[:])
 
         warm = sb.tile([P, 1], F32, name="warm")
         nc.scalar.activation(warm[:], identity[:, 0:1], ACT.Exp)
 
-        query2_bf = interleave("query2_bf", query2_raw, "query2_bf")
-        query_bf = interleave("query_bf", query_raw, "query_bf")
+        query2_bf = interleave("query2_bf", query2_raw)
+        query_bf = interleave("query_bf", query_raw)
+        gout_bf = interleave("gout_bf", gout_raw)
 
-        key_words = gather("key_words", key_word_pool, U16, "key_words")
-        key_scales = gather("key_scales", key_scale_pool, U8, "key_scales")
+        key_words = gather("key_words", key_word_pool, U16)
+        key_scales = gather("key_scales", key_scale_pool, U8)
         query2_mx = quantize("query2", query2_bf)
         query_mx = quantize("query", query_bf)
         b = product("b", query2_mx, key_words, key_scales)
         a = product("a", query_mx, key_words, key_scales)
-        size_rows = ps.tile([Q, PACK, P], F32, name="size_rows")
-        for j in range(PACK):
-            nc.tensor.transpose(size_rows[:, j, :], size_cols[:, j : j + 1].to_broadcast([P, P]), identity[:])
-        val_words = gather("val_words", val_word_pool, U16, "query_bf")
+        val_scales = gather("val_scales", val_scale_pool, U8)
+        gout_mx = quantize("gout", gout_bf)
 
         b1 = sb.tile([Q, I], F32, name="b1")
         nc.scalar.activation(b1[:], b[:], ACT.Copy, bias=1.0)
-        gout_bf = interleave("gout_bf", gout_raw, "key_words")
-        s = sb.tile([Q, I], F32, name="s", tag="wide", align_bytes=64)
+        s = sb.tile([Q, I], F32, name="s")
         nc.vector.tensor_tensor(s[:], a[:], b1[:], ALU.mult)
-        gout_mx = quantize("gout", gout_bf)
-        neg_s = sb.tile([Q, I], F32, name="neg_s", tag="key_words", align_bytes=64)
         neg_max = sb.tile([Q, 1], F32, name="neg_max")
-        nc.vector.tensor_scalar(neg_s[:], s[:], -1.0, None, ALU.mult, ALU.min, accum_out=neg_max[:])
+        nc.vector.tensor_reduce(neg_max[:], s[:], mybir.AxisListType.X, ALU.max, negate=True)
         p = sb.tile([Q, I], F32, name="p")
         z = sb.tile([Q, 1], F32, name="z")
-        nc.scalar.activation(p[:], neg_s[:], ACT.Exp, bias=neg_max[:], scale=-1.0, accum_out=z[:])
+        nc.scalar.activation(p[:], s[:], ACT.Exp, bias=neg_max[:], accum_out=z[:])
 
-        val_scales = gather("val_scales", val_scale_pool, U8, "wide")
+        val_words = gather("val_words", val_word_pool, U16)
         c0 = product("c0", gout_mx, val_words, val_scales)
 
         rz = sb.tile([Q, 1], F32, name="rz")
         nc.vector.reciprocal(rz[:], z[:])
         pn = sb.tile([Q, I], F32, name="pn")
         nc.scalar.activation(pn[:], p[:], ACT.Copy, scale=rz[:])
-        pn_size = sb.tile([Q, P, PACK], F32, name="pn_size")
-        nc.vector.scalar_tensor_tensor(pn_size[:], p[:].rearrange("q (n j) -> q n j", j=PACK), rz[:],
-                                       size_rows[:].rearrange("q j n -> q n j"), ALU.mult, ALU.mult)
+        p_size = sb.tile([Q, P, PACK], F32, name="p_size")
+        nc.vector.tensor_tensor(p_size[:], p[:].rearrange("q (n j) -> q n j", j=PACK),
+                                size_rows[:].rearrange("q j n -> q n j"), ALU.mult)
         direct = sb.tile([Q, I], F32, name="direct")
         direct_sum = sb.tile([Q, 1], F32, name="direct_sum")
-        nc.vector.scalar_tensor_tensor(direct[:], c0[:], -512.0, pn_size[:].rearrange("q n j -> q (n j)"),
+        nc.vector.scalar_tensor_tensor(direct[:], c0[:], rz[:], p_size[:].rearrange("q n j -> q (n j)"),
                                        ALU.mult, ALU.mult, accum_out=direct_sum[:])
-        ds = sb.tile([Q, I], F32, name="ds")
-        nc.vector.scalar_tensor_tensor(ds[:], pn[:], direct_sum[:], direct[:], ALU.mult, ALU.subtract)
-        nc.vector.tensor_tensor(scattered[:].indirect(offsets[:]), ds[:], b1[:], ALU.mult)
+        neg_ds = sb.tile([Q, I], F32, name="neg_ds")
+        nc.vector.scalar_tensor_tensor(neg_ds[:], pn[:], direct_sum[:], direct[:], ALU.mult, ALU.subtract)
+        nc.vector.tensor_tensor(scattered[:].indirect(offsets[:]), neg_ds[:], b1[:], ALU.mult)
 
-        start = 0
-        for k, width in enumerate(OUT_WIDTHS):
-            cols = slice(start, start + width)
-            start = start + width
-            total = sb.tile([Q, width], F32, name="total%d" % k)
-            nc.vector.tensor_tensor(total[:], scattered[:, cols], old_sb[:, cols], ALU.add)
+        for k in range(T // OUT_CHUNK):
+            cols = slice(k * OUT_CHUNK, (k + 1) * OUT_CHUNK)
+            total = sb.tile([Q, OUT_CHUNK], F32, name="total%d" % k)
+            nc.vector.scalar_tensor_tensor(total[:], scattered[:, cols], -512.0, old_sb[:, cols], ALU.mult, ALU.add)
             nc.sync.dma_start(out[:, cols], total[:])

@@ -3,7 +3,7 @@ from contextlib import ExitStack
 import concourse.mybir as mybir
 from concourse.masks import make_identity
 
-D, E, T, I, Q = 512, 512, 2048, 512, 128
+D, T, I, Q = 512, 2048, 512, 128
 FLOPS = 3 * 2 * D * Q * I
 
 F32 = mybir.dt.float32
@@ -19,96 +19,114 @@ ACT = mybir.ActivationFunctionType
 
 P = 128
 PACK = 4
+QUADRANT = 32
+BLOCKS = D // 32
+SLOTS_A_COLUMN = 16
+HALF = I // 2
+GRADIENT_SCALE = 512.0
 OUT_CHUNK = 256
 
 
-def tile_attend_bproductscore_a_s_kernel(tc, query, query2, keys_words, keys_scales, gout, vals_words, vals_scales, size, old, offs, out):
+def tile_attend_bproductscore_a_s_kernel(
+    tc, query, query2, keys_words, keys_scales, gout, vals_words, vals_scales, size, old, offs, out
+):
     nc = tc.nc
     with ExitStack() as ctx:
         sb = ctx.enter_context(tc.tile_pool(name="sb", bufs=1))
         ps = ctx.enter_context(tc.psum_pool(name="ps", bufs=1))
 
-        offsets = sb.tile([P, I // 16], U16, name="offsets")
+        offsets = sb.tile([P, I // SLOTS_A_COLUMN], U16, name="offsets")
         nc.sync.dma_start(offsets[:], offs)
 
-        def scale_pool(name):
-            pool = sb.tile([P, T], U8, name=name)
-            nc.vector.memset(pool[:].bitcast(I32), 0)
-            return pool
+        def zeroed_scale_table(name):
+            table = sb.tile([P, T], U8, name=name)
+            nc.vector.memset(table[:].bitcast(I32), 0)
+            return table
 
-        def load_scales(pool, scales):
+        def load_scales(table, scales):
             for r in range(4):
-                nc.sync.dma_start(pool[r:P:32, :].bitcast(I32), scales[0, r:16:4, :].bitcast(I32))
+                nc.sync.dma_start(table[r:P:QUADRANT, :].bitcast(I32), scales[0, r:BLOCKS:4, :].bitcast(I32))
 
         def load_words(name, words):
-            pool = sb.tile([P, T], U16, name=name)
-            nc.sync.dma_start(pool[:].bitcast(I32), words[0].bitcast(I32))
-            return pool
+            table = sb.tile([P, T], U16, name=name)
+            nc.sync.dma_start(table[:].bitcast(I32), words[0].bitcast(I32))
+            return table
 
         def load_rows(name, x):
             raw = sb.tile([P, PACK, Q], F32, name=name)
-            nc.sync.dma_start(raw[:], x.rearrange("(p j) q -> p j q", j=PACK))
+            nc.sync.dma_start(raw[:], x.rearrange("(p t) q -> p t q", t=PACK))
             return raw
 
         def interleave(name, raw):
             grouped = sb.tile([P, Q, PACK], BF16, name=name, align_bytes=64)
-            nc.scalar.copy(grouped[:].rearrange("p (c i) j -> p c j i", i=4), raw[:].rearrange("p j (c i) -> p c j i", i=4))
+            nc.scalar.copy(grouped[:], raw[:].rearrange("p t q -> p q t"))
             return grouped
 
         def quantize(name, grouped):
             codes = sb.tile([P, Q], U32, name=name + "_codes", align_bytes=64)
             scales = sb.tile([P, Q], U8, name=name + "_scales", align_bytes=64)
-            nc.vector.quantize_mx(out=codes[:].bitcast(FP8X4), scales=scales[:], in_=grouped[:].rearrange("p q j -> p (q j)"))
+            nc.vector.quantize_mx(
+                out=codes[:].bitcast(FP8X4), scales=scales[:], in_=grouped[:].rearrange("p q t -> p (q t)")
+            )
             return codes, scales
 
-        def gather(name, pool, dtype):
+        def gather(name, table, dtype):
             listed = sb.tile([P, I], dtype, name=name, align_bytes=64)
-            nc.vector.tensor_copy(listed[:], pool[:].indirect(offsets[:]))
+            nc.vector.tensor_copy(listed[:], table[:].indirect(offsets[:]))
             return listed
 
-        def product(name, rows, words, scales):
-            bank = ps.tile([Q, I], F32, name=name)
-            nc.tensor.matmul_mx(out=bank[:], lhsT=rows[0][:].bitcast(FP8X4), lhsT_scale=rows[1][:],
-                                rhs=words[:].bitcast(FP4X4), rhs_scale=scales[:], start=True, stop=True)
-            return bank
+        def product(result, rows_mx, words, scales):
+            codes, row_scales = rows_mx
+            nc.tensor.matmul_mx(
+                out=result,
+                lhsT=codes[:].bitcast(FP8X4),
+                lhsT_scale=row_scales[:],
+                rhs=words.bitcast(FP4X4),
+                rhs_scale=scales,
+                start=True,
+                stop=True,
+            )
 
-        key_scale_pool = scale_pool("key_scale_pool")
-        val_scale_pool = scale_pool("val_scale_pool")
+        key_scale_table = zeroed_scale_table("key_scale_table")
+        val_scale_table = zeroed_scale_table("val_scale_table")
         scattered = sb.tile([Q, T], F32, name="scattered")
-        nc.vector.memset(scattered[:].bitcast(I32), 0)
+        nc.vector.memset(scattered[:], 0.0)
 
-        size_cols = sb.tile([P, PACK], F32, name="size_cols")
-        nc.sync.dma_start(size_cols[:], size.rearrange("o (p j) -> (o p) j", j=PACK))
-        key_word_pool = load_words("key_word_pool", keys_words)
+        load_scales(key_scale_table, keys_scales)
+        key_word_table = load_words("key_word_table", keys_words)
         query2_raw = load_rows("query2_raw", query2)
-        load_scales(key_scale_pool, keys_scales)
         query_raw = load_rows("query_raw", query)
-        load_scales(val_scale_pool, vals_scales)
+        load_scales(val_scale_table, vals_scales)
         gout_raw = load_rows("gout_raw", gout)
-        val_word_pool = load_words("val_word_pool", vals_words)
+        val_word_table = load_words("val_word_table", vals_words)
         old_sb = sb.tile([Q, T], F32, name="old_sb")
         nc.sync.dma_start(old_sb[:], old)
 
         identity = sb.tile([P, P], F32, name="identity")
         make_identity(nc, identity[:])
+        size_cols = sb.tile([P, PACK], F32, name="size_cols")
+        nc.gpsimd.dma_start(size_cols[:], size.rearrange("o (n j) -> (o n) j", j=PACK))
         size_rows = ps.tile([Q, PACK, P], F32, name="size_rows")
         for j in range(PACK):
             nc.tensor.transpose(size_rows[:, j, :], size_cols[:, j : j + 1].to_broadcast([P, P]), identity[:])
 
-        warm = sb.tile([P, 1], F32, name="warm")
-        nc.scalar.activation(warm[:], identity[:, 0:1], ACT.Exp)
+        exp_warm_up = sb.tile([P, 1], F32, name="exp_warm_up")
+        nc.scalar.activation(exp_warm_up[:], identity[:, 0:1], ACT.Exp)
 
         query2_bf = interleave("query2_bf", query2_raw)
         query_bf = interleave("query_bf", query_raw)
         gout_bf = interleave("gout_bf", gout_raw)
 
-        key_words = gather("key_words", key_word_pool, U16)
-        key_scales = gather("key_scales", key_scale_pool, U8)
+        key_scales = gather("key_scales", key_scale_table, U8)
+        key_words = gather("key_words", key_word_table, U16)
         query2_mx = quantize("query2", query2_bf)
         query_mx = quantize("query", query_bf)
-        b = product("b", query2_mx, key_words, key_scales)
-        a = product("a", query_mx, key_words, key_scales)
-        val_scales = gather("val_scales", val_scale_pool, U8)
+        b = ps.tile([Q, I], F32, name="b")
+        product(b[:], query2_mx, key_words[:], key_scales[:])
+        a = ps.tile([Q, I], F32, name="a")
+        product(a[:], query_mx, key_words[:], key_scales[:])
+
+        val_scales = gather("val_scales", val_scale_table, U8)
         gout_mx = quantize("gout", gout_bf)
 
         b1 = sb.tile([Q, I], F32, name="b1")
@@ -121,26 +139,38 @@ def tile_attend_bproductscore_a_s_kernel(tc, query, query2, keys_words, keys_sca
         z = sb.tile([Q, 1], F32, name="z")
         nc.scalar.activation(p[:], s[:], ACT.Exp, bias=neg_max[:], accum_out=z[:])
 
-        val_words = gather("val_words", val_word_pool, U16)
-        c0 = product("c0", gout_mx, val_words, val_scales)
+        val_words = sb.tile([P, I], U16, name="val_words", align_bytes=64)
+        c0 = ps.tile([Q, I], F32, name="c0")
+        for start in range(0, I, HALF):
+            slots = slice(start, start + HALF)
+            list_cols = slice(start // SLOTS_A_COLUMN, (start + HALF) // SLOTS_A_COLUMN)
+            nc.vector.tensor_copy(val_words[:, slots], val_word_table[:].indirect(offsets[:, list_cols]))
+            product(c0[:, slots], gout_mx, val_words[:, slots], val_scales[:, slots])
 
         rz = sb.tile([Q, 1], F32, name="rz")
+        p_size = sb.tile([Q, I], F32, name="p_size")
         nc.vector.reciprocal(rz[:], z[:])
         pn = sb.tile([Q, I], F32, name="pn")
         nc.scalar.activation(pn[:], p[:], ACT.Copy, scale=rz[:])
-        p_size = sb.tile([Q, P, PACK], F32, name="p_size")
-        nc.vector.tensor_tensor(p_size[:], p[:].rearrange("q (n j) -> q n j", j=PACK),
-                                size_rows[:].rearrange("q j n -> q n j"), ALU.mult)
+        nc.vector.tensor_tensor(
+            p_size[:].rearrange("q (n j) -> q n j", j=PACK),
+            p[:].rearrange("q (n j) -> q n j", j=PACK),
+            size_rows[:].rearrange("q j n -> q n j"),
+            ALU.mult,
+        )
         direct = sb.tile([Q, I], F32, name="direct")
         direct_sum = sb.tile([Q, 1], F32, name="direct_sum")
-        nc.vector.scalar_tensor_tensor(direct[:], c0[:], rz[:], p_size[:].rearrange("q n j -> q (n j)"),
-                                       ALU.mult, ALU.mult, accum_out=direct_sum[:])
+        nc.vector.scalar_tensor_tensor(
+            direct[:], c0[:], rz[:], p_size[:], ALU.mult, ALU.mult, accum_out=direct_sum[:]
+        )
         neg_ds = sb.tile([Q, I], F32, name="neg_ds")
         nc.vector.scalar_tensor_tensor(neg_ds[:], pn[:], direct_sum[:], direct[:], ALU.mult, ALU.subtract)
         nc.vector.tensor_tensor(scattered[:].indirect(offsets[:]), neg_ds[:], b1[:], ALU.mult)
 
-        for k in range(T // OUT_CHUNK):
-            cols = slice(k * OUT_CHUNK, (k + 1) * OUT_CHUNK)
-            total = sb.tile([Q, OUT_CHUNK], F32, name="total%d" % k)
-            nc.vector.scalar_tensor_tensor(total[:], scattered[:, cols], -512.0, old_sb[:, cols], ALU.mult, ALU.add)
+        for start in range(0, T, OUT_CHUNK):
+            cols = slice(start, start + OUT_CHUNK)
+            total = sb.tile([Q, OUT_CHUNK], F32, name="total%d" % start)
+            nc.vector.scalar_tensor_tensor(
+                total[:], scattered[:, cols], -GRADIENT_SCALE, old_sb[:, cols], ALU.mult, ALU.add
+            )
             nc.sync.dma_start(out[:, cols], total[:])

from contextlib import ExitStack

import concourse.mybir as mybir
from concourse.masks import make_identity

D, T, I, Q = 512, 2048, 512, 128
FLOPS = 3 * 2 * D * Q * I

F32 = mybir.dt.float32
BF16 = mybir.dt.bfloat16
I32 = mybir.dt.int32
U32 = mybir.dt.uint32
U16 = mybir.dt.uint16
U8 = mybir.dt.uint8
FP8X4 = mybir.dt.float8_e4m3fn_x4
FP4X4 = mybir.dt.float4_e2m1fn_x4
ALU = mybir.AluOpType
ACT = mybir.ActivationFunctionType

P = 128
PACK = 4
QUADRANT = 32
BLOCKS = D // 32
SLOTS_A_COLUMN = 16
HALF = I // 2
GRADIENT_SCALE = 512.0
OUT_CHUNK = 256


def tile_attend_bproductscore_a_s_kernel(
    tc, query, query2, keys_words, keys_scales, gout, vals_words, vals_scales, size, old, offs, out
):
    nc = tc.nc
    with ExitStack() as ctx:
        sb = ctx.enter_context(tc.tile_pool(name="sb", bufs=1))
        ps = ctx.enter_context(tc.psum_pool(name="ps", bufs=1))

        offsets = sb.tile([P, I // SLOTS_A_COLUMN], U16, name="offsets")
        nc.sync.dma_start(offsets[:], offs)

        def zeroed_scale_table(name):
            table = sb.tile([P, T], U8, name=name)
            nc.vector.memset(table[:].bitcast(I32), 0)
            return table

        def load_scales(table, scales):
            for r in range(4):
                nc.sync.dma_start(table[r:P:QUADRANT, :].bitcast(I32), scales[0, r:BLOCKS:4, :].bitcast(I32))

        def load_words(name, words):
            table = sb.tile([P, T], U16, name=name)
            nc.sync.dma_start(table[:].bitcast(I32), words[0].bitcast(I32))
            return table

        def load_rows(name, x):
            raw = sb.tile([P, PACK, Q], F32, name=name)
            nc.sync.dma_start(raw[:], x.rearrange("(p t) q -> p t q", t=PACK))
            return raw

        def interleave(name, raw):
            grouped = sb.tile([P, Q, PACK], BF16, name=name, align_bytes=64)
            nc.scalar.copy(grouped[:], raw[:].rearrange("p t q -> p q t"))
            return grouped

        def quantize(name, grouped):
            codes = sb.tile([P, Q], U32, name=name + "_codes", align_bytes=64)
            scales = sb.tile([P, Q], U8, name=name + "_scales", align_bytes=64)
            nc.vector.quantize_mx(
                out=codes[:].bitcast(FP8X4), scales=scales[:], in_=grouped[:].rearrange("p q t -> p (q t)")
            )
            return codes, scales

        def gather(name, table, dtype):
            listed = sb.tile([P, I], dtype, name=name, align_bytes=64)
            nc.vector.tensor_copy(listed[:], table[:].indirect(offsets[:]))
            return listed

        def product(result, rows_mx, words, scales):
            codes, row_scales = rows_mx
            nc.tensor.matmul_mx(
                out=result,
                lhsT=codes[:].bitcast(FP8X4),
                lhsT_scale=row_scales[:],
                rhs=words.bitcast(FP4X4),
                rhs_scale=scales,
                start=True,
                stop=True,
            )

        key_scale_table = zeroed_scale_table("key_scale_table")
        val_scale_table = zeroed_scale_table("val_scale_table")
        scattered = sb.tile([Q, T], F32, name="scattered")
        nc.vector.memset(scattered[:], 0.0)

        load_scales(key_scale_table, keys_scales)
        key_word_table = load_words("key_word_table", keys_words)
        query2_raw = load_rows("query2_raw", query2)
        query_raw = load_rows("query_raw", query)
        load_scales(val_scale_table, vals_scales)
        gout_raw = load_rows("gout_raw", gout)
        val_word_table = load_words("val_word_table", vals_words)
        old_sb = sb.tile([Q, T], F32, name="old_sb")
        nc.sync.dma_start(old_sb[:], old)

        identity = sb.tile([P, P], F32, name="identity")
        make_identity(nc, identity[:])
        size_cols = sb.tile([P, PACK], F32, name="size_cols")
        nc.gpsimd.dma_start(size_cols[:], size.rearrange("o (n j) -> (o n) j", j=PACK))
        size_rows = ps.tile([Q, PACK, P], F32, name="size_rows")
        for j in range(PACK):
            nc.tensor.transpose(size_rows[:, j, :], size_cols[:, j : j + 1].to_broadcast([P, P]), identity[:])

        exp_warm_up = sb.tile([P, 1], F32, name="exp_warm_up")
        nc.scalar.activation(exp_warm_up[:], identity[:, 0:1], ACT.Exp)

        query2_bf = interleave("query2_bf", query2_raw)
        query_bf = interleave("query_bf", query_raw)
        gout_bf = interleave("gout_bf", gout_raw)

        key_scales = gather("key_scales", key_scale_table, U8)
        key_words = gather("key_words", key_word_table, U16)
        query2_mx = quantize("query2", query2_bf)
        query_mx = quantize("query", query_bf)
        b = ps.tile([Q, I], F32, name="b")
        product(b[:], query2_mx, key_words[:], key_scales[:])
        a = ps.tile([Q, I], F32, name="a")
        product(a[:], query_mx, key_words[:], key_scales[:])

        val_scales = gather("val_scales", val_scale_table, U8)
        gout_mx = quantize("gout", gout_bf)

        b1 = sb.tile([Q, I], F32, name="b1")
        nc.scalar.activation(b1[:], b[:], ACT.Copy, bias=1.0)
        s = sb.tile([Q, I], F32, name="s")
        nc.vector.tensor_tensor(s[:], a[:], b1[:], ALU.mult)
        neg_max = sb.tile([Q, 1], F32, name="neg_max")
        nc.vector.tensor_reduce(neg_max[:], s[:], mybir.AxisListType.X, ALU.max, negate=True)
        p = sb.tile([Q, I], F32, name="p")
        z = sb.tile([Q, 1], F32, name="z")
        nc.scalar.activation(p[:], s[:], ACT.Exp, bias=neg_max[:], accum_out=z[:])

        val_words = sb.tile([P, I], U16, name="val_words", align_bytes=64)
        c0 = ps.tile([Q, I], F32, name="c0")
        for start in range(0, I, HALF):
            slots = slice(start, start + HALF)
            list_cols = slice(start // SLOTS_A_COLUMN, (start + HALF) // SLOTS_A_COLUMN)
            nc.vector.tensor_copy(val_words[:, slots], val_word_table[:].indirect(offsets[:, list_cols]))
            product(c0[:, slots], gout_mx, val_words[:, slots], val_scales[:, slots])

        rz = sb.tile([Q, 1], F32, name="rz")
        p_size = sb.tile([Q, I], F32, name="p_size")
        nc.vector.reciprocal(rz[:], z[:])
        pn = sb.tile([Q, I], F32, name="pn")
        nc.scalar.activation(pn[:], p[:], ACT.Copy, scale=rz[:])
        nc.vector.tensor_tensor(
            p_size[:].rearrange("q (n j) -> q n j", j=PACK),
            p[:].rearrange("q (n j) -> q n j", j=PACK),
            size_rows[:].rearrange("q j n -> q n j"),
            ALU.mult,
        )
        direct = sb.tile([Q, I], F32, name="direct")
        direct_sum = sb.tile([Q, 1], F32, name="direct_sum")
        nc.vector.scalar_tensor_tensor(
            direct[:], c0[:], rz[:], p_size[:], ALU.mult, ALU.mult, accum_out=direct_sum[:]
        )
        neg_ds = sb.tile([Q, I], F32, name="neg_ds")
        nc.vector.scalar_tensor_tensor(neg_ds[:], pn[:], direct_sum[:], direct[:], ALU.mult, ALU.subtract)
        nc.vector.tensor_tensor(scattered[:].indirect(offsets[:]), neg_ds[:], b1[:], ALU.mult)

        for start in range(0, T, OUT_CHUNK):
            cols = slice(start, start + OUT_CHUNK)
            total = sb.tile([Q, OUT_CHUNK], F32, name="total%d" % start)
            nc.vector.scalar_tensor_tensor(
                total[:], scattered[:, cols], -GRADIENT_SCALE, old_sb[:, cols], ALU.mult, ALU.add
            )
            nc.sync.dma_start(out[:, cols], total[:])
